import numpy as np
import ml_dtypes


def mxq(x, axis, fmt="e4m3"):
    dtype, down = {"e4m3": (ml_dtypes.float8_e4m3fn, 7), "e5m2": (ml_dtypes.float8_e5m2, 14)}[fmt]
    v = np.moveaxis(np.asarray(x, np.float32).astype(ml_dtypes.bfloat16).astype(np.float64), axis, -1)
    blocks = v.reshape(v.shape[:-1] + (-1, 32))
    amax = np.abs(blocks).max(-1, keepdims=True)
    byte = np.maximum(np.where(amax > 0, np.frexp(amax)[1] - 1 + 127, 0) - down, 1)
    scale = np.exp2(byte - 127.0)
    codes = (blocks / scale).astype(np.float32).astype(dtype).astype(np.float64)
    return np.moveaxis((codes * scale).reshape(v.shape), -1, axis)


WIDE = False


def mx_kscale(k):
    if not WIDE:
        return np.ones(k)
    levels = np.array([10, -10, 5, -5, 0])
    if k % 512:
        return np.exp2(np.random.permutation(np.resize(levels, k // 32))).repeat(32)
    a = np.empty((k // 512, 16))
    for p in range(k // 512):
        a[p, :8] = np.random.permutation(np.resize(levels, 8))
        for g in range(8):
            far = levels[np.abs(levels - a[p, g]) >= 10]
            a[p, g + 8] = far[np.random.randint(len(far))]
    return np.exp2(a.ravel()).repeat(32)


def f64(x):
    return np.asarray(x).astype(np.float64)


def striped(idx):
    return np.tile(np.asarray(idx).reshape(-1, 16).T, (8, 1)).astype(np.uint16)


def unstriped(offs):
    return offs[:16].T.reshape(-1).astype(np.int64)


E2M1 = np.array([0.0, 0.5, 1.0, 1.5, 2.0, 3.0, 4.0, 6.0, -0.0, -0.5, -1.0, -1.5, -2.0, -3.0, -4.0, -6.0])


def pack_weight(w, fmt):
    k, n = w.shape
    w = f64(np.asarray(w, np.float32).astype(ml_dtypes.bfloat16)).reshape(k // 32, 32, n)
    amax = np.abs(w).max(1)
    if fmt == "e4m3":
        byte = np.frexp(amax)[1] - 1 + 127 - 7
    else:
        mant, ex = np.frexp(amax / 6.0)
        byte = np.where(mant > 0.5, ex, ex - 1) + 127
    byte = np.clip(np.where(amax > 0, byte, 1), 1, 254)
    scaled = (w * np.exp2(127.0 - byte)[:, None, :]).reshape(k, n).astype(np.float32)
    by_word = np.ascontiguousarray(scaled.reshape(k // 512, 128, 4, n).transpose(0, 1, 3, 2))
    if fmt == "e4m3":
        words = by_word.astype(ml_dtypes.float8_e4m3fn).view(np.uint8)
    else:
        c = by_word.astype(ml_dtypes.float4_e2m1fn).view(np.uint8) & 0xF
        words = (c[..., 0::2] | (c[..., 1::2] << 4)).reshape(k // 512, 128, 2 * n)
    return np.ascontiguousarray(words), np.ascontiguousarray(byte.astype(np.uint8).reshape(k // 512, 16, n))


def unpack_weight(words, scales, fmt):
    g, _, n = scales.shape
    words = np.ascontiguousarray(words).reshape(g, 128, n, -1)
    if fmt == "e4m3":
        vals = words.view(ml_dtypes.float8_e4m3fn).astype(np.float64)
    else:
        nib = np.empty((g, 128, n, 4), np.uint8)
        nib[..., 0::2] = words & 0xF
        nib[..., 1::2] = words >> 4
        vals = E2M1[nib]
    vals = vals * np.repeat(np.exp2(scales.astype(np.float64) - 127.0), 8, axis=1)[..., None]
    return vals.transpose(0, 1, 3, 2).reshape(g * 512, n)


D, E, T, I, G, U, Q = 512, 512, 4096, 1024, 64, 512, 128


def setup_inputs():
    n = np.random.standard_normal
    idx = np.random.permutation(T)[:I]
    idx2 = np.random.permutation(U)[:G]
    fd = mx_kscale(D)
    fe = mx_kscale(E)
    keysp = pack_weight(n((D, T)) / fd[:, None], "e2m1")
    valsp = pack_weight(n((E, T)) / fe[:, None], "e2m1")
    return {
        "query": (n((D, Q)) * 0.8 / np.sqrt(D) * fd[:, None]).astype(np.float32),
        "keys_words": keysp[0],
        "keys_scales": keysp[1],
        "ptab": (0.5 * n((Q, U)) - 4.3).astype(np.float32),
        "gout": (n((E, Q)) * 1 / np.sqrt(E) * fe[:, None]).astype(np.float32),
        "vals_words": valsp[0],
        "vals_scales": valsp[1],
        "old": (0.5 * n((Q, U))).astype(np.float32),
        "offs": striped(idx),
        "offs2": striped(idx2),
    }


def reference(query, keys_words, keys_scales, ptab, gout, vals_words, vals_scales, old, offs, offs2):
    idx = unstriped(offs)
    idx2 = unstriped(offs2)
    keysu = unpack_weight(keys_words, keys_scales, "e2m1")
    valsu = unpack_weight(vals_words, vals_scales, "e2m1")
    queryq = mxq(f64(query), 0, "e4m3")
    keysidxg = keysu[:, idx]
    a = queryq.T @ keysidxg
    p = np.exp(a - np.max(a, axis=1, keepdims=True))
    z = np.sum(p, axis=1, keepdims=True)
    goutq = mxq(f64(gout), 0, "e4m3")
    valsidxg = valsu[:, idx]
    c0 = goutq.T @ valsidxg
    s = p.reshape(Q, G, I // G).sum(axis=2) / z
    m1 = (p * c0).reshape(Q, G, I // G).sum(axis=2) / z
    tp = np.exp(f64(ptab)[:, idx2])
    dtp = m1 / np.square(1.0 + s / tp) * (-1.0) * s / np.square(tp) * (-1.0)
    gs = dtp * tp * 64.0
    gf = np.zeros((Q, U))
    gf[:, idx2] = gs
    y = f64(old) + gf
    return y

@@ -1,0 +1,187 @@
+from contextlib import ExitStack
+
+import concourse.mybir as mybir
+from concourse.masks import make_identity
+
+D, E, T, I, G, U, Q = 512, 512, 4096, 1024, 64, 512, 128
+FLOPS = 2 * Q * I * (D + E)
+
+F32 = mybir.dt.float32
+BF16 = mybir.dt.bfloat16
+I32 = mybir.dt.int32
+U32 = mybir.dt.uint32
+U16 = mybir.dt.uint16
+U8 = mybir.dt.uint8
+FP8X4 = mybir.dt.float8_e4m3fn_x4
+FP4X4 = mybir.dt.float4_e2m1fn_x4
+ALU = mybir.AluOpType
+ACT = mybir.ActivationFunctionType
+AXIS = mybir.AxisListType
+
+P = 128
+PACK = 4
+PAGE = I // G
+HALF = 512
+HALVES = I // HALF
+HALF_PAGES = HALF // PAGE
+PAIRS = PAGE // 2
+SPREAD = 8
+
+
+def tile_attend_bpagecap_kernel(tc, query, keys_words, keys_scales, ptab, gout, vals_words, vals_scales, old,
+                                 offs, offs2, out):
+    nc = tc.nc
+    with ExitStack() as ctx:
+        sb = ctx.enter_context(tc.tile_pool(name="sb", bufs=1))
+        reuse = ctx.enter_context(tc.tile_pool(name="reuse", bufs=1))
+        ps = ctx.enter_context(tc.psum_pool(name="ps", bufs=1))
+
+        slots = sb.tile([P, I // 16], U16, name="slots")
+        pages = sb.tile([P, G // 16], U16, name="pages")
+        nc.sync.dma_start(slots[:], offs)
+
+        def load_scales(window, scales):
+            nc.vector.memset(window[:].bitcast(I32), 0)
+            nc.scalar.dma_start(window[0:P:SPREAD, :].bitcast(I32), scales[0].bitcast(I32))
+
+        def load_words(name, words, tag):
+            window = sb.tile([P, T], U16, name=name + "_word_window", tag=tag, align_bytes=64)
+            nc.sync.dma_start(window[:].bitcast(I32), words[0].bitcast(I32))
+            return window
+
+        def load_rows(name, rows, tag):
+            raw = sb.tile([P, PACK, Q], F32, name=name + "_raw", tag=tag, align_bytes=64)
+            nc.sync.dma_start(raw[:], rows.rearrange("(p t) q -> p t q", t=PACK))
+            return raw
+
+        def empty_plane(name):
+            plane = sb.tile([P, I], U8, name=name + "_scale_plane", align_bytes=64)
+            nc.vector.memset(plane[:].bitcast(I32), 0)
+            return plane
+
+        def gather_scales(picked, window, plane, queue):
+            nc.vector.tensor_copy(picked[:], window[:].indirect(slots[:]))
+            for quad in range(4):
+                queue.dma_start(plane[32 * quad:32 * quad + 4, :].bitcast(I32),
+                                picked[32 * quad:32 * quad + 32:SPREAD, :].bitcast(I32))
+
+        def quantise(name, raw, codes):
+            woven = sb.tile([P, Q, PACK], BF16, name=name + "_woven", align_bytes=64)
+            nc.scalar.copy(woven[:], raw[:].rearrange("p t q -> p q t"))
+            plane = sb.tile([P, Q], U8, name=name + "_plane", align_bytes=64)
+            nc.vector.quantize_mx(out=codes[:].bitcast(FP8X4), scales=plane[:],
+                                  in_=woven[:].rearrange("p q t -> p (q t)"))
+            return codes, plane
+
+        def product(name, picked, window, plane, rows, h):
+            cols = HALF // 16
+            nc.vector.tensor_copy(picked, window[:].indirect(slots[:, h * cols:(h + 1) * cols]))
+            bank = ps.tile([P, HALF], F32, name="%s_bank%d" % (name, h))
+            nc.tensor.matmul_mx(out=bank[:], lhsT=rows[0][:].bitcast(FP8X4), lhsT_scale=rows[1][:],
+                                rhs=picked.bitcast(FP4X4), rhs_scale=plane[:, h * HALF:(h + 1) * HALF],
+                                start=True, stop=True)
+            return bank
+
+        key_scale_window = reuse.tile([P, T], U8, name="key_scale_window", offset=0, align_bytes=64)
+        val_scale_window = sb.tile([P, T], U8, name="val_scale_window", align_bytes=64)
+        load_scales(key_scale_window, keys_scales)
+        load_scales(val_scale_window, vals_scales)
+        nc.sync.dma_start(pages[:], offs2)
+        log_caps = sb.tile([P, U], F32, name="log_caps")
+        nc.sync.dma_start(log_caps[:], ptab)
+        query_raw = load_rows("query", query, "slot_c")
+        key_word_window = load_words("key", keys_words, "slot_a")
+        gout_raw = load_rows("gout", gout, "slot_d")
+
+        key_plane = empty_plane("key")
+        val_plane = empty_plane("val")
+        placed = sb.tile([P, U], F32, name="placed")
+        nc.vector.memset(placed[:], 0.0)
+        ident = sb.tile([P, P], F32, name="ident")
+        make_identity(nc, ident[:])
+
+        log_cap = sb.tile([P, G], F32, name="log_cap")
+        nc.vector.tensor_copy(log_cap[:], log_caps[:].indirect(pages[:]))
+        cap = sb.tile([P, G], F32, name="cap")
+        nc.scalar.activation(cap[:], log_cap[:], ACT.Exp)
+
+        key_scale_picked = sb.tile([P, I], U8, name="key_scale_picked", align_bytes=64)
+        gather_scales(key_scale_picked, key_scale_window, key_plane, nc.scalar)
+        query_mx = quantise("query", query_raw, reuse.tile([P, Q], U32, name="query_codes", offset=0, align_bytes=64))
+        val_word_window = load_words("val", vals_words, "slot_c")
+
+        key_picked = [reuse.tile([P, HALF], U16, name="key_picked%d" % h, offset=1024 * (h + 1), align_bytes=64)
+                      for h in range(HALVES)]
+        scores = [product("key", key_picked[h][:], key_word_window, key_plane, query_mx, h) for h in range(HALVES)]
+        neg_max0 = sb.tile([P, 1], F32, name="neg_max0")
+        nc.vector.tensor_reduce(neg_max0[:], scores[0][:], AXIS.X, ALU.max, negate=True)
+        gout_mx = quantise("gout", gout_raw, reuse.tile([P, Q], U32, name="gout_codes", offset=1024, align_bytes=64))
+        old_sb = sb.tile([P, U], F32, name="old_sb", tag="slot_d", align_bytes=64)
+        nc.sync.dma_start(old_sb[:], old)
+        max1 = sb.tile([P, 1], F32, name="max1")
+        nc.vector.tensor_reduce(max1[:], scores[1][:], AXIS.X, ALU.max)
+        excess = sb.tile([P, 1], F32, name="excess")
+        nc.scalar.activation(excess[:], max1[:], ACT.Relu, bias=neg_max0[:])
+        neg_max = sb.tile([P, 1], F32, name="neg_max")
+        nc.scalar.activation(neg_max[:], excess[:], ACT.Identity, bias=neg_max0[:], scale=-1.0)
+
+        weights = sb.tile([P, PAIRS, G, 2], F32, name="weights")
+        half_sums = [sb.tile([P, 1], F32, name="half_sum%d" % h) for h in range(HALVES)]
+        for h in range(HALVES):
+            nc.scalar.activation(weights[:, :, h * HALF_PAGES:(h + 1) * HALF_PAGES, :],
+                                 scores[h][:].rearrange("p (g a b) -> p a g b", a=PAIRS, b=2),
+                                 ACT.Exp, bias=neg_max[:], accum_out=half_sums[h][:])
+        row_sum = sb.tile([P, 1], F32, name="row_sum")
+        nc.scalar.activation(row_sum[:], half_sums[0][:], ACT.Identity, bias=half_sums[1][:])
+
+        turned = ps.tile([P, P], F32, name="turned")
+        for a in range(PAIRS):
+            nc.tensor.matmul(turned[:], weights[:, a, :, :].rearrange("p g b -> p (g b)"), ident[:],
+                             is_transpose=True, start=(a == 0), stop=(a == PAIRS - 1))
+        turned_sb = sb.tile([P, P], F32, name="turned_sb")
+        nc.scalar.copy(turned_sb[:], turned[:])
+        pair_sums = ps.tile([P, P], F32, name="pair_sums")
+        nc.tensor.transpose(pair_sums[:], turned_sb[:], ident[:])
+
+        val_scale_picked = reuse.tile([P, I], U8, name="val_scale_picked", offset=1536, align_bytes=64)
+        gather_scales(val_scale_picked, val_scale_window, val_plane, nc.sync)
+        val_picked = reuse.tile([P, I], U16, name="val_picked", offset=2560, align_bytes=64)
+        grads = [product("val", val_picked[:, h * HALF:(h + 1) * HALF], val_word_window, val_plane, gout_mx, h)
+                 for h in range(HALVES)]
+
+        moment = sb.tile([P, G], F32, name="moment")
+        weighted = [sb.tile([P, HALF_PAGES, PAIRS, 2], F32, name="weighted%d" % h) for h in range(HALVES)]
+
+        def weigh(h):
+            nc.vector.tensor_tensor(weighted[h][:], grads[h][:].rearrange("p (g a b) -> p g a b", a=PAIRS, b=2),
+                                    weights[:, :, h * HALF_PAGES:(h + 1) * HALF_PAGES, :].rearrange("p a g b -> p g a b"),
+                                    ALU.mult)
+
+        def sum_pages(h):
+            nc.vector.tensor_reduce(moment[:, h * HALF_PAGES:(h + 1) * HALF_PAGES],
+                                    weighted[h][:].rearrange("p g a b -> p g (a b)"), AXIS.X, ALU.add)
+
+        share = sb.tile([P, G], F32, name="share")
+        denom = sb.tile([P, G], F32, name="denom")
+        inv = sb.tile([P, G], F32, name="inv")
+        numer = sb.tile([P, G], F32, name="numer")
+        once = sb.tile([P, G], F32, name="once")
+        factor = sb.tile([P, G], F32, name="factor")
+
+        nc.vector.tensor_reduce(share[:], pair_sums[:].rearrange("p (g b) -> p g b", b=2), AXIS.X, ALU.add)
+        nc.vector.scalar_tensor_tensor(denom[:], cap[:], row_sum[:], share[:], ALU.mult, ALU.add)
+        nc.vector.scalar_tensor_tensor(numer[:], share[:], 64.0, cap[:], ALU.mult, ALU.mult)
+        nc.vector.reciprocal(inv[:], denom[:])
+        weigh(0)
+        nc.vector.tensor_tensor(once[:], numer[:], inv[:], ALU.mult)
+        weigh(1)
+        sum_pages(0)
+        nc.vector.tensor_tensor(factor[:], once[:], inv[:], ALU.mult)
+        sum_pages(1)
+        nc.vector.tensor_tensor(placed[:].indirect(pages[:]), moment[:], factor[:], ALU.mult)
+
+        result = sb.tile([P, U], F32, name="result")
+        for h, queue in enumerate((nc.sync, nc.scalar)):
+            cols = slice(h * U // 2, (h + 1) * U // 2)
+            nc.vector.tensor_tensor(result[:, cols], placed[:, cols], old_sb[:, cols], ALU.add)
+            queue.dma_start(out[:, cols], result[:, cols])

@@ -1,7 +1,6 @@
 from contextlib import ExitStack
 
 import concourse.mybir as mybir
-from concourse.masks import make_identity
 
 D, E, T, I, G, U, Q = 512, 512, 4096, 1024, 64, 512, 128
 FLOPS = 2 * Q * I * (D + E)
@@ -34,90 +33,106 @@ def tile_attend_bpagecap_kernel(tc, query, keys_words, keys_scales, ptab, gout, 
     with ExitStack() as ctx:
         sb = ctx.enter_context(tc.tile_pool(name="sb", bufs=1))
         reuse = ctx.enter_context(tc.tile_pool(name="reuse", bufs=1))
+        late = ctx.enter_context(tc.tile_pool(name="late", bufs=1))
         ps = ctx.enter_context(tc.psum_pool(name="ps", bufs=1))
 
         slots = sb.tile([P, I // 16], U16, name="slots")
         pages = sb.tile([P, G // 16], U16, name="pages")
         nc.sync.dma_start(slots[:], offs)
 
+        def half_list(h):
+            cols = HALF // 16
+            return slots[:, h * cols:(h + 1) * cols]
+
         def load_scales(window, scales):
             nc.vector.memset(window[:].bitcast(I32), 0)
             nc.scalar.dma_start(window[0:P:SPREAD, :].bitcast(I32), scales[0].bitcast(I32))
 
-        def load_words(name, words, tag):
-            window = sb.tile([P, T], U16, name=name + "_word_window", tag=tag, align_bytes=64)
+        def load_words(window, words):
             nc.sync.dma_start(window[:].bitcast(I32), words[0].bitcast(I32))
             return window
 
-        def load_rows(name, rows, tag):
-            raw = sb.tile([P, PACK, Q], F32, name=name + "_raw", tag=tag, align_bytes=64)
+        def load_rows(raw, rows):
             nc.sync.dma_start(raw[:], rows.rearrange("(p t) q -> p t q", t=PACK))
             return raw
 
         def empty_plane(name):
             plane = sb.tile([P, I], U8, name=name + "_scale_plane", align_bytes=64)
             nc.vector.memset(plane[:].bitcast(I32), 0)
-            return plane
+            return [plane[:, h * HALF:(h + 1) * HALF] for h in range(HALVES)]
 
-        def gather_scales(picked, window, plane, queue):
-            nc.vector.tensor_copy(picked[:], window[:].indirect(slots[:]))
-            for quad in range(4):
-                queue.dma_start(plane[32 * quad:32 * quad + 4, :].bitcast(I32),
-                                picked[32 * quad:32 * quad + 32:SPREAD, :].bitcast(I32))
+        def gather_scales(picked, window, planes, queues):
+            for h in range(HALVES):
+                nc.vector.tensor_copy(picked[h][:], window[:].indirect(half_list(h)))
+                for quad in range(4):
+                    queue = queues[quad % len(queues)]
+                    queue.dma_start(planes[h][32 * quad:32 * quad + 4, :].bitcast(I32),
+                                    picked[h][32 * quad:32 * quad + 32:SPREAD, :].bitcast(I32))
 
-        def quantise(name, raw, codes):
+        def weave(name, raw):
             woven = sb.tile([P, Q, PACK], BF16, name=name + "_woven", align_bytes=64)
             nc.scalar.copy(woven[:], raw[:].rearrange("p t q -> p q t"))
+            return woven
+
+        def quantise(name, woven, codes):
             plane = sb.tile([P, Q], U8, name=name + "_plane", align_bytes=64)
             nc.vector.quantize_mx(out=codes[:].bitcast(FP8X4), scales=plane[:],
                                   in_=woven[:].rearrange("p q t -> p (q t)"))
             return codes, plane
 
         def product(name, picked, window, plane, rows, h):
-            cols = HALF // 16
-            nc.vector.tensor_copy(picked, window[:].indirect(slots[:, h * cols:(h + 1) * cols]))
+            nc.vector.tensor_copy(picked, window[:].indirect(half_list(h)))
             bank = ps.tile([P, HALF], F32, name="%s_bank%d" % (name, h))
             nc.tensor.matmul_mx(out=bank[:], lhsT=rows[0][:].bitcast(FP8X4), lhsT_scale=rows[1][:],
-                                rhs=picked.bitcast(FP4X4), rhs_scale=plane[:, h * HALF:(h + 1) * HALF],
+                                rhs=picked.bitcast(FP4X4), rhs_scale=plane[h],
                                 start=True, stop=True)
             return bank
 
         key_scale_window = reuse.tile([P, T], U8, name="key_scale_window", offset=0, align_bytes=64)
         val_scale_window = sb.tile([P, T], U8, name="val_scale_window", align_bytes=64)
+        zeros = sb.tile([P, P], F32, name="zeros", tag="zeros_then_key_words", align_bytes=64)
+        nc.vector.memset(zeros[:], 0.0)
         load_scales(key_scale_window, keys_scales)
+        ident = sb.tile([P, P], F32, name="ident")
+        nc.vector.tensor_copy(ident[:], zeros[:])
+        warm = sb.tile([P, 1], F32, name="warm")
+        nc.scalar.activation(warm[:], ident[:, 0:1], ACT.Exp)
+        nc.gpsimd.affine_select(out=ident[:], in_=ident[:], compare_op=ALU.not_equal, fill=1.0, base=0,
+                                pattern=[[-1, P]], channel_multiplier=1)
         load_scales(val_scale_window, vals_scales)
         nc.sync.dma_start(pages[:], offs2)
         log_caps = sb.tile([P, U], F32, name="log_caps")
         nc.sync.dma_start(log_caps[:], ptab)
-        query_raw = load_rows("query", query, "slot_c")
-        key_word_window = load_words("key", keys_words, "slot_a")
-        gout_raw = load_rows("gout", gout, "slot_d")
+        query_raw = load_rows(sb.tile([P, PACK, Q], F32, name="query_raw", tag="rows"), query)
+        key_word_window = load_words(
+            sb.tile([P, T], U16, name="key_word_window", tag="zeros_then_key_words", align_bytes=64), keys_words)
 
         key_plane = empty_plane("key")
         val_plane = empty_plane("val")
         placed = sb.tile([P, U], F32, name="placed")
         nc.vector.memset(placed[:], 0.0)
-        ident = sb.tile([P, P], F32, name="ident")
-        make_identity(nc, ident[:])
 
         log_cap = sb.tile([P, G], F32, name="log_cap")
         nc.vector.tensor_copy(log_cap[:], log_caps[:].indirect(pages[:]))
         cap = sb.tile([P, G], F32, name="cap")
         nc.scalar.activation(cap[:], log_cap[:], ACT.Exp)
 
-        key_scale_picked = sb.tile([P, I], U8, name="key_scale_picked", align_bytes=64)
-        gather_scales(key_scale_picked, key_scale_window, key_plane, nc.scalar)
-        query_mx = quantise("query", query_raw, reuse.tile([P, Q], U32, name="query_codes", offset=0, align_bytes=64))
-        val_word_window = load_words("val", vals_words, "slot_c")
+        query_woven = weave("query", query_raw)
+        gout_raw = load_rows(sb.tile([P, PACK, Q], F32, name="gout_raw", tag="rows"), gout)
+        key_scale_picked = [late.tile([P, HALF], U8, name="key_scale_picked0", offset=2 * T - HALF // 2, align_bytes=64),
+                            sb.tile([P, HALF], U8, name="key_scale_picked1", align_bytes=64)]
+        gather_scales(key_scale_picked, key_scale_window, key_plane, (nc.sync, nc.scalar))
+        query_mx = quantise("query", query_woven, reuse.tile([P, Q], U32, name="query_codes", offset=0, align_bytes=64))
+        val_word_window = load_words(late.tile([P, T], U16, name="val_word_window", offset=0, align_bytes=64), vals_words)
+        old_sb = late.tile([P, U], F32, name="old_sb", offset=2 * T, align_bytes=64)
+        nc.sync.dma_start(old_sb[:], old)
 
-        key_picked = [reuse.tile([P, HALF], U16, name="key_picked%d" % h, offset=1024 * (h + 1), align_bytes=64)
+        key_picked = [reuse.tile([P, HALF], U16, name="key_picked%d" % h, offset=1024 + 1280 * h, align_bytes=64)
                       for h in range(HALVES)]
         scores = [product("key", key_picked[h][:], key_word_window, key_plane, query_mx, h) for h in range(HALVES)]
         neg_max0 = sb.tile([P, 1], F32, name="neg_max0")
         nc.vector.tensor_reduce(neg_max0[:], scores[0][:], AXIS.X, ALU.max, negate=True)
-        gout_mx = quantise("gout", gout_raw, reuse.tile([P, Q], U32, name="gout_codes", offset=1024, align_bytes=64))
-        old_sb = sb.tile([P, U], F32, name="old_sb", tag="slot_d", align_bytes=64)
-        nc.sync.dma_start(old_sb[:], old)
+        gout_mx = quantise("gout", weave("gout", gout_raw), reuse.tile([P, Q], U32, name="gout_codes", offset=1024, align_bytes=64))
         max1 = sb.tile([P, 1], F32, name="max1")
         nc.vector.tensor_reduce(max1[:], scores[1][:], AXIS.X, ALU.max)
         excess = sb.tile([P, 1], F32, name="excess")
@@ -134,18 +149,22 @@ def tile_attend_bpagecap_kernel(tc, query, keys_words, keys_scales, ptab, gout, 
         row_sum = sb.tile([P, 1], F32, name="row_sum")
         nc.scalar.activation(row_sum[:], half_sums[0][:], ACT.Identity, bias=half_sums[1][:])
 
+
         turned = ps.tile([P, P], F32, name="turned")
         for a in range(PAIRS):
             nc.tensor.matmul(turned[:], weights[:, a, :, :].rearrange("p g b -> p (g b)"), ident[:],
                              is_transpose=True, start=(a == 0), stop=(a == PAIRS - 1))
         turned_sb = sb.tile([P, P], F32, name="turned_sb")
         nc.scalar.copy(turned_sb[:], turned[:])
+        warm_root = sb.tile([P, 1], F32, name="warm_root")
+        nc.scalar.activation(warm_root[:], turned_sb[:, 0:1], ACT.Abs_reciprocal_sqrt)
         pair_sums = ps.tile([P, P], F32, name="pair_sums")
         nc.tensor.transpose(pair_sums[:], turned_sb[:], ident[:])
 
-        val_scale_picked = reuse.tile([P, I], U8, name="val_scale_picked", offset=1536, align_bytes=64)
-        gather_scales(val_scale_picked, val_scale_window, val_plane, nc.sync)
-        val_picked = reuse.tile([P, I], U16, name="val_picked", offset=2560, align_bytes=64)
+        val_scale_picked = [reuse.tile([P, HALF], U8, name="val_scale_picked%d" % h, offset=2048 + HALF * h, align_bytes=64)
+                            for h in range(HALVES)]
+        gather_scales(val_scale_picked, val_scale_window, val_plane, (nc.sync,))
+        val_picked = reuse.tile([P, I], U16, name="val_picked", offset=3072, align_bytes=64)
         grads = [product("val", val_picked[:, h * HALF:(h + 1) * HALF], val_word_window, val_plane, gout_mx, h)
                  for h in range(HALVES)]
 
@@ -169,12 +188,14 @@ def tile_attend_bpagecap_kernel(tc, query, keys_words, keys_scales, ptab, gout, 
         factor = sb.tile([P, G], F32, name="factor")
 
         nc.vector.tensor_reduce(share[:], pair_sums[:].rearrange("p (g b) -> p g b", b=2), AXIS.X, ALU.add)
+        weigh(0)
         nc.vector.scalar_tensor_tensor(denom[:], cap[:], row_sum[:], share[:], ALU.mult, ALU.add)
         nc.vector.scalar_tensor_tensor(numer[:], share[:], 64.0, cap[:], ALU.mult, ALU.mult)
-        nc.vector.reciprocal(inv[:], denom[:])
-        weigh(0)
-        nc.vector.tensor_tensor(once[:], numer[:], inv[:], ALU.mult)
+        root = sb.tile([P, G], F32, name="root")
+        nc.scalar.activation(root[:], denom[:], ACT.Abs_reciprocal_sqrt)
+        nc.scalar.activation(inv[:], root[:], ACT.Square)
         weigh(1)
+        nc.vector.tensor_tensor(once[:], numer[:], inv[:], ALU.mult)
         sum_pages(0)
         nc.vector.tensor_tensor(factor[:], once[:], inv[:], ALU.mult)
         sum_pages(1)

@@ -46,7 +46,7 @@ def tile_attend_bpagecap_kernel(tc, query, keys_words, keys_scales, ptab, gout, 
 
         def load_scales(window, scales):
             nc.vector.memset(window[:].bitcast(I32), 0)
-            nc.scalar.dma_start(window[0:P:SPREAD, :].bitcast(I32), scales[0].bitcast(I32))
+            nc.sync.dma_start(window[0:P:SPREAD, :].bitcast(I32), scales[0].bitcast(I32))
 
         def load_words(window, words):
             nc.sync.dma_start(window[:].bitcast(I32), words[0].bitcast(I32))
@@ -57,9 +57,10 @@ def tile_attend_bpagecap_kernel(tc, query, keys_words, keys_scales, ptab, gout, 
             return raw
 
         def empty_plane(name):
-            plane = sb.tile([P, I], U8, name=name + "_scale_plane", align_bytes=64)
-            nc.vector.memset(plane[:].bitcast(I32), 0)
-            return [plane[:, h * HALF:(h + 1) * HALF] for h in range(HALVES)]
+            planes = [sb.tile([P, HALF], U8, name="%s_scale_plane%d" % (name, h), align_bytes=64) for h in range(HALVES)]
+            for plane in planes:
+                nc.vector.memset(plane[:].bitcast(I32), 0)
+            return [plane[:] for plane in planes]
 
         def gather_scales(picked, window, planes, queues):
             for h in range(HALVES):
@@ -74,65 +75,69 @@ def tile_attend_bpagecap_kernel(tc, query, keys_words, keys_scales, ptab, gout, 
             nc.scalar.copy(woven[:], raw[:].rearrange("p t q -> p q t"))
             return woven
 
-        def quantise(name, woven, codes):
+        def quantise(name, woven):
+            codes = sb.tile([P, Q], U32, name=name + "_codes", align_bytes=64)
             plane = sb.tile([P, Q], U8, name=name + "_plane", align_bytes=64)
             nc.vector.quantize_mx(out=codes[:].bitcast(FP8X4), scales=plane[:],
                                   in_=woven[:].rearrange("p q t -> p (q t)"))
             return codes, plane
 
-        def product(name, picked, window, plane, rows, h):
+        def product(tag, picked, window, plane, rows, h):
             nc.vector.tensor_copy(picked, window[:].indirect(half_list(h)))
-            bank = ps.tile([P, HALF], F32, name="%s_bank%d" % (name, h))
+            bank = ps.tile([P, HALF], F32, name="bank", tag=tag)
             nc.tensor.matmul_mx(out=bank[:], lhsT=rows[0][:].bitcast(FP8X4), lhsT_scale=rows[1][:],
                                 rhs=picked.bitcast(FP4X4), rhs_scale=plane[h],
                                 start=True, stop=True)
             return bank
 
-        key_scale_window = reuse.tile([P, T], U8, name="key_scale_window", offset=0, align_bytes=64)
+        seed = sb.tile([P, 1], F32, name="seed")
+        nc.gpsimd.memset(seed[:], 0.0)
+        warm = sb.tile([P, 1], F32, name="warm")
+        nc.scalar.activation(warm[:], seed[:], ACT.Exp)
+        key_scale_window = sb.tile([P, T], U8, name="key_scale_window", align_bytes=64)
         val_scale_window = sb.tile([P, T], U8, name="val_scale_window", align_bytes=64)
         zeros = sb.tile([P, P], F32, name="zeros", tag="zeros_then_key_words", align_bytes=64)
-        nc.vector.memset(zeros[:], 0.0)
+        nc.gpsimd.memset(zeros[:], 0.0)
         load_scales(key_scale_window, keys_scales)
         ident = sb.tile([P, P], F32, name="ident")
         nc.vector.tensor_copy(ident[:], zeros[:])
-        warm = sb.tile([P, 1], F32, name="warm")
-        nc.scalar.activation(warm[:], ident[:, 0:1], ACT.Exp)
         nc.gpsimd.affine_select(out=ident[:], in_=ident[:], compare_op=ALU.not_equal, fill=1.0, base=0,
                                 pattern=[[-1, P]], channel_multiplier=1)
-        load_scales(val_scale_window, vals_scales)
-        nc.sync.dma_start(pages[:], offs2)
-        log_caps = sb.tile([P, U], F32, name="log_caps")
-        nc.sync.dma_start(log_caps[:], ptab)
         query_raw = load_rows(sb.tile([P, PACK, Q], F32, name="query_raw", tag="rows"), query)
+        nc.sync.dma_start(pages[:], offs2)
+        log_caps = sb.tile([P, U], F32, name="log_caps", tag="caps_then_plane", align_bytes=64)
+        nc.sync.dma_start(log_caps[:], ptab)
         key_word_window = load_words(
             sb.tile([P, T], U16, name="key_word_window", tag="zeros_then_key_words", align_bytes=64), keys_words)
 
+        load_scales(val_scale_window, vals_scales)
         key_plane = empty_plane("key")
-        val_plane = empty_plane("val")
-        placed = sb.tile([P, U], F32, name="placed")
-        nc.vector.memset(placed[:], 0.0)
 
+        query_mx = quantise("query", weave("query", query_raw))
         log_cap = sb.tile([P, G], F32, name="log_cap")
         nc.vector.tensor_copy(log_cap[:], log_caps[:].indirect(pages[:]))
-        cap = sb.tile([P, G], F32, name="cap")
-        nc.scalar.activation(cap[:], log_cap[:], ACT.Exp)
+        inv_cap = sb.tile([P, G], F32, name="inv_cap")
+        nc.scalar.activation(inv_cap[:], log_cap[:], ACT.Exp, scale=-1.0)
 
-        query_woven = weave("query", query_raw)
+        val_planes = sb.tile([P, I], U8, name="val_scale_plane", tag="caps_then_plane", align_bytes=64)
+        nc.gpsimd.memset(val_planes[:].bitcast(I32), 0)
+        val_plane = [val_planes[:, h * HALF:(h + 1) * HALF] for h in range(HALVES)]
         gout_raw = load_rows(sb.tile([P, PACK, Q], F32, name="gout_raw", tag="rows"), gout)
         key_scale_picked = [late.tile([P, HALF], U8, name="key_scale_picked0", offset=2 * T - HALF // 2, align_bytes=64),
                             sb.tile([P, HALF], U8, name="key_scale_picked1", align_bytes=64)]
         gather_scales(key_scale_picked, key_scale_window, key_plane, (nc.sync, nc.scalar))
-        query_mx = quantise("query", query_woven, reuse.tile([P, Q], U32, name="query_codes", offset=0, align_bytes=64))
         val_word_window = load_words(late.tile([P, T], U16, name="val_word_window", offset=0, align_bytes=64), vals_words)
         old_sb = late.tile([P, U], F32, name="old_sb", offset=2 * T, align_bytes=64)
         nc.sync.dma_start(old_sb[:], old)
 
-        key_picked = [reuse.tile([P, HALF], U16, name="key_picked%d" % h, offset=1024 + 1280 * h, align_bytes=64)
-                      for h in range(HALVES)]
-        scores = [product("key", key_picked[h][:], key_word_window, key_plane, query_mx, h) for h in range(HALVES)]
+        key_picked = reuse.tile([P, I], U16, name="key_picked", offset=1024, align_bytes=64)
+        scores = [product("scores%d" % h, key_picked[:, h * HALF:(h + 1) * HALF], key_word_window, key_plane, query_mx, h)
+                  for h in range(HALVES)]
+        gout_mx = quantise("gout", weave("gout", gout_raw))
+        placed = sb.tile([P, U], F32, name="placed", tag="rows")
+        nc.gpsimd.memset(placed[:], 0.0)
         neg_max0 = sb.tile([P, 1], F32, name="neg_max0")
         nc.vector.tensor_reduce(neg_max0[:], scores[0][:], AXIS.X, ALU.max, negate=True)
-        gout_mx = quantise("gout", weave("gout", gout_raw), reuse.tile([P, Q], U32, name="gout_codes", offset=1024, align_bytes=64))
         max1 = sb.tile([P, 1], F32, name="max1")
         nc.vector.tensor_reduce(max1[:], scores[1][:], AXIS.X, ALU.max)
         excess = sb.tile([P, 1], F32, name="excess")
@@ -141,31 +146,35 @@ def tile_attend_bpagecap_kernel(tc, query, keys_words, keys_scales, ptab, gout, 
         nc.scalar.activation(neg_max[:], excess[:], ACT.Identity, bias=neg_max0[:], scale=-1.0)
 
         weights = sb.tile([P, PAIRS, G, 2], F32, name="weights")
-        half_sums = [sb.tile([P, 1], F32, name="half_sum%d" % h) for h in range(HALVES)]
-        for h in range(HALVES):
-            nc.scalar.activation(weights[:, :, h * HALF_PAGES:(h + 1) * HALF_PAGES, :],
-                                 scores[h][:].rearrange("p (g a b) -> p a g b", a=PAIRS, b=2),
-                                 ACT.Exp, bias=neg_max[:], accum_out=half_sums[h][:])
+        part_sums = sb.tile([P, 2, HALVES], F32, name="part_sums")
+        for part in range(2):
+            pairs = slice(part * PAIRS // 2, (part + 1) * PAIRS // 2)
+            for h in range(HALVES):
+                nc.scalar.activation(weights[:, pairs, h * HALF_PAGES:(h + 1) * HALF_PAGES, :],
+                                     scores[h][:].rearrange("p (g a b) -> p a g b", a=PAIRS, b=2)[:, pairs],
+                                     ACT.Exp, bias=neg_max[:], accum_out=part_sums[:, part, h:h + 1])
         row_sum = sb.tile([P, 1], F32, name="row_sum")
-        nc.scalar.activation(row_sum[:], half_sums[0][:], ACT.Identity, bias=half_sums[1][:])
+        part_copy = sb.tile([P, 2, HALVES], F32, name="part_copy")
+        nc.scalar.activation(part_copy[:], part_sums[:], ACT.Identity, accum_out=row_sum[:])
 
 
-        turned = ps.tile([P, P], F32, name="turned")
+        turned = ps.tile([P, P], F32, name="turned", tag="turned")
         for a in range(PAIRS):
             nc.tensor.matmul(turned[:], weights[:, a, :, :].rearrange("p g b -> p (g b)"), ident[:],
                              is_transpose=True, start=(a == 0), stop=(a == PAIRS - 1))
         turned_sb = sb.tile([P, P], F32, name="turned_sb")
         nc.scalar.copy(turned_sb[:], turned[:])
         warm_root = sb.tile([P, 1], F32, name="warm_root")
-        nc.scalar.activation(warm_root[:], turned_sb[:, 0:1], ACT.Abs_reciprocal_sqrt)
+        nc.scalar.activation(warm_root[:], turned_sb[:, 0:1], ACT.Abs_reciprocal_sqrt, bias=row_sum[:])
         pair_sums = ps.tile([P, P], F32, name="pair_sums")
         nc.tensor.transpose(pair_sums[:], turned_sb[:], ident[:])
 
-        val_scale_picked = [reuse.tile([P, HALF], U8, name="val_scale_picked%d" % h, offset=2048 + HALF * h, align_bytes=64)
+        val_scale_picked = [reuse.tile([P, HALF], U8, name="val_scale_picked%d" % h, offset=1088 + HALF * h, align_bytes=64)
                             for h in range(HALVES)]
         gather_scales(val_scale_picked, val_scale_window, val_plane, (nc.sync,))
-        val_picked = reuse.tile([P, I], U16, name="val_picked", offset=3072, align_bytes=64)
-        grads = [product("val", val_picked[:, h * HALF:(h + 1) * HALF], val_word_window, val_plane, gout_mx, h)
+        val_picked = [reuse.tile([P, HALF], U16, name="val_picked%d" % h, offset=64 + 2048 * h, align_bytes=64)
+                      for h in range(HALVES)]
+        grads = [product("grads%d" % h, val_picked[h][:], val_word_window, val_plane, gout_mx, h)
                  for h in range(HALVES)]
 
         moment = sb.tile([P, G], F32, name="moment")
@@ -181,23 +190,21 @@ def tile_attend_bpagecap_kernel(tc, query, keys_words, keys_scales, ptab, gout, 
                                     weighted[h][:].rearrange("p g a b -> p g (a b)"), AXIS.X, ALU.add)
 
         share = sb.tile([P, G], F32, name="share")
-        denom = sb.tile([P, G], F32, name="denom")
+        ratio = reuse.tile([P, G], F32, name="ratio", offset=64 + 2048, align_bytes=64)
+        root = sb.tile([P, G], F32, name="root")
         inv = sb.tile([P, G], F32, name="inv")
-        numer = sb.tile([P, G], F32, name="numer")
-        once = sb.tile([P, G], F32, name="once")
+        inv_square = sb.tile([P, G], F32, name="inv_square")
         factor = sb.tile([P, G], F32, name="factor")
 
         nc.vector.tensor_reduce(share[:], pair_sums[:].rearrange("p (g b) -> p g b", b=2), AXIS.X, ALU.add)
         weigh(0)
-        nc.vector.scalar_tensor_tensor(denom[:], cap[:], row_sum[:], share[:], ALU.mult, ALU.add)
-        nc.vector.scalar_tensor_tensor(numer[:], share[:], 64.0, cap[:], ALU.mult, ALU.mult)
-        root = sb.tile([P, G], F32, name="root")
-        nc.scalar.activation(root[:], denom[:], ACT.Abs_reciprocal_sqrt)
+        nc.vector.tensor_tensor(ratio[:], share[:], inv_cap[:], ALU.mult)
+        nc.scalar.activation(root[:], ratio[:], ACT.Abs_reciprocal_sqrt, bias=row_sum[:])
         nc.scalar.activation(inv[:], root[:], ACT.Square)
+        nc.scalar.activation(inv_square[:], inv[:], ACT.Square)
         weigh(1)
-        nc.vector.tensor_tensor(once[:], numer[:], inv[:], ALU.mult)
         sum_pages(0)
-        nc.vector.tensor_tensor(factor[:], once[:], inv[:], ALU.mult)
+        nc.vector.scalar_tensor_tensor(factor[:], ratio[:], 64.0, inv_square[:], ALU.mult, ALU.mult)
         sum_pages(1)
         nc.vector.tensor_tensor(placed[:].indirect(pages[:]), moment[:], factor[:], ALU.mult)
 

@@ -94,7 +94,7 @@ def tile_attend_bpagecap_kernel(tc, query, keys_words, keys_scales, ptab, gout, 
         nc.gpsimd.memset(seed[:], 0.0)
         warm = sb.tile([P, 1], F32, name="warm")
         nc.scalar.activation(warm[:], seed[:], ACT.Exp)
-        key_scale_window = sb.tile([P, T], U8, name="key_scale_window", align_bytes=64)
+        key_scale_window = late.tile([P, T], U8, name="key_scale_window", offset=2 * T - T // 2, align_bytes=64)
         val_scale_window = sb.tile([P, T], U8, name="val_scale_window", align_bytes=64)
         zeros = sb.tile([P, P], F32, name="zeros", tag="zeros_then_key_words", align_bytes=64)
         nc.gpsimd.memset(zeros[:], 0.0)
@@ -123,8 +123,7 @@ def tile_attend_bpagecap_kernel(tc, query, keys_words, keys_scales, ptab, gout, 
         nc.gpsimd.memset(val_planes[:].bitcast(I32), 0)
         val_plane = [val_planes[:, h * HALF:(h + 1) * HALF] for h in range(HALVES)]
         gout_raw = load_rows(sb.tile([P, PACK, Q], F32, name="gout_raw", tag="rows"), gout)
-        key_scale_picked = [late.tile([P, HALF], U8, name="key_scale_picked0", offset=2 * T - HALF // 2, align_bytes=64),
-                            sb.tile([P, HALF], U8, name="key_scale_picked1", align_bytes=64)]
+        key_scale_picked = [sb.tile([P, HALF], U8, name="key_scale_picked%d" % h, align_bytes=64) for h in range(HALVES)]
         gather_scales(key_scale_picked, key_scale_window, key_plane, (nc.sync, nc.scalar))
         val_word_window = load_words(late.tile([P, T], U16, name="val_word_window", offset=0, align_bytes=64), vals_words)
         old_sb = late.tile([P, U], F32, name="old_sb", offset=2 * T, align_bytes=64)
@@ -169,12 +168,12 @@ def tile_attend_bpagecap_kernel(tc, query, keys_words, keys_scales, ptab, gout, 
         pair_sums = ps.tile([P, P], F32, name="pair_sums")
         nc.tensor.transpose(pair_sums[:], turned_sb[:], ident[:])
 
-        val_scale_picked = [reuse.tile([P, HALF], U8, name="val_scale_picked%d" % h, offset=1088 + HALF * h, align_bytes=64)
-                            for h in range(HALVES)]
+        val_scale_picked = [sb.tile([P, HALF], U8, name="val_scale_picked0", align_bytes=64),
+                            reuse.tile([P, HALF], U8, name="val_scale_picked1", offset=1088, align_bytes=64)]
         gather_scales(val_scale_picked, val_scale_window, val_plane, (nc.sync,))
         val_picked = [reuse.tile([P, HALF], U16, name="val_picked%d" % h, offset=64 + 2048 * h, align_bytes=64)
                       for h in range(HALVES)]
-        grads = [product("grads%d" % h, val_picked[h][:], val_word_window, val_plane, gout_mx, h)
+        grads = [product(("grads0", "turned")[h], val_picked[h][:], val_word_window, val_plane, gout_mx, h)
                  for h in range(HALVES)]
 
         moment = sb.tile([P, G], F32, name="moment")
@@ -190,7 +189,7 @@ def tile_attend_bpagecap_kernel(tc, query, keys_words, keys_scales, ptab, gout, 
                                     weighted[h][:].rearrange("p g a b -> p g (a b)"), AXIS.X, ALU.add)
 
         share = sb.tile([P, G], F32, name="share")
-        ratio = reuse.tile([P, G], F32, name="ratio", offset=64 + 2048, align_bytes=64)
+        ratio = sb.tile([P, G], F32, name="ratio")
         root = sb.tile([P, G], F32, name="root")
         inv = sb.tile([P, G], F32, name="inv")
         inv_square = sb.tile([P, G], F32, name="inv_square")

@@ -60,7 +60,7 @@ def tile_attend_bpagecap_kernel(tc, query, keys_words, keys_scales, ptab, gout, 
             planes = [sb.tile([P, HALF], U8, name="%s_scale_plane%d" % (name, h), align_bytes=64) for h in range(HALVES)]
             for plane in planes:
                 nc.vector.memset(plane[:].bitcast(I32), 0)
-            return [plane[:] for plane in planes]
+            return planes
 
         def gather_scales(picked, window, planes, queues):
             for h in range(HALVES):
@@ -86,7 +86,7 @@ def tile_attend_bpagecap_kernel(tc, query, keys_words, keys_scales, ptab, gout, 
             nc.vector.tensor_copy(picked, window[:].indirect(half_list(h)))
             bank = ps.tile([P, HALF], F32, name="bank", tag=tag)
             nc.tensor.matmul_mx(out=bank[:], lhsT=rows[0][:].bitcast(FP8X4), lhsT_scale=rows[1][:],
-                                rhs=picked.bitcast(FP4X4), rhs_scale=plane[h],
+                                rhs=picked.bitcast(FP4X4), rhs_scale=plane[h][:],
                                 start=True, stop=True)
             return bank
 
@@ -94,7 +94,7 @@ def tile_attend_bpagecap_kernel(tc, query, keys_words, keys_scales, ptab, gout, 
         nc.gpsimd.memset(seed[:], 0.0)
         warm = sb.tile([P, 1], F32, name="warm")
         nc.scalar.activation(warm[:], seed[:], ACT.Exp)
-        key_scale_window = late.tile([P, T], U8, name="key_scale_window", offset=2 * T - T // 2, align_bytes=64)
+        key_scale_window = sb.tile([P, T], U8, name="key_scale_window", align_bytes=64)
         val_scale_window = sb.tile([P, T], U8, name="val_scale_window", align_bytes=64)
         zeros = sb.tile([P, P], F32, name="zeros", tag="zeros_then_key_words", align_bytes=64)
         nc.gpsimd.memset(zeros[:], 0.0)
@@ -105,13 +105,16 @@ def tile_attend_bpagecap_kernel(tc, query, keys_words, keys_scales, ptab, gout, 
                                 pattern=[[-1, P]], channel_multiplier=1)
         query_raw = load_rows(sb.tile([P, PACK, Q], F32, name="query_raw", tag="rows"), query)
         nc.sync.dma_start(pages[:], offs2)
-        log_caps = sb.tile([P, U], F32, name="log_caps", tag="caps_then_plane", align_bytes=64)
+        log_caps = sb.tile([P, U], F32, name="log_caps")
         nc.sync.dma_start(log_caps[:], ptab)
         key_word_window = load_words(
             sb.tile([P, T], U16, name="key_word_window", tag="zeros_then_key_words", align_bytes=64), keys_words)
 
         load_scales(val_scale_window, vals_scales)
         key_plane = empty_plane("key")
+        val_plane = empty_plane("val")
+        placed = sb.tile([P, U], F32, name="placed")
+        nc.vector.memset(placed[:], 0.0)
 
         query_mx = quantise("query", weave("query", query_raw))
         log_cap = sb.tile([P, G], F32, name="log_cap")
@@ -119,11 +122,9 @@ def tile_attend_bpagecap_kernel(tc, query, keys_words, keys_scales, ptab, gout, 
         inv_cap = sb.tile([P, G], F32, name="inv_cap")
         nc.scalar.activation(inv_cap[:], log_cap[:], ACT.Exp, scale=-1.0)
 
-        val_planes = sb.tile([P, I], U8, name="val_scale_plane", tag="caps_then_plane", align_bytes=64)
-        nc.gpsimd.memset(val_planes[:].bitcast(I32), 0)
-        val_plane = [val_planes[:, h * HALF:(h + 1) * HALF] for h in range(HALVES)]
         gout_raw = load_rows(sb.tile([P, PACK, Q], F32, name="gout_raw", tag="rows"), gout)
-        key_scale_picked = [sb.tile([P, HALF], U8, name="key_scale_picked%d" % h, align_bytes=64) for h in range(HALVES)]
+        key_scale_picked = [late.tile([P, HALF], U8, name="key_scale_picked0", offset=2 * T - HALF // 2, align_bytes=64),
+                            sb.tile([P, HALF], U8, name="key_scale_picked1", align_bytes=64)]
         gather_scales(key_scale_picked, key_scale_window, key_plane, (nc.sync, nc.scalar))
         val_word_window = load_words(late.tile([P, T], U16, name="val_word_window", offset=0, align_bytes=64), vals_words)
         old_sb = late.tile([P, U], F32, name="old_sb", offset=2 * T, align_bytes=64)
@@ -133,8 +134,6 @@ def tile_attend_bpagecap_kernel(tc, query, keys_words, keys_scales, ptab, gout, 
         scores = [product("scores%d" % h, key_picked[:, h * HALF:(h + 1) * HALF], key_word_window, key_plane, query_mx, h)
                   for h in range(HALVES)]
         gout_mx = quantise("gout", weave("gout", gout_raw))
-        placed = sb.tile([P, U], F32, name="placed", tag="rows")
-        nc.gpsimd.memset(placed[:], 0.0)
         neg_max0 = sb.tile([P, 1], F32, name="neg_max0")
         nc.vector.tensor_reduce(neg_max0[:], scores[0][:], AXIS.X, ALU.max, negate=True)
         max1 = sb.tile([P, 1], F32, name="max1")
@@ -168,12 +167,12 @@ def tile_attend_bpagecap_kernel(tc, query, keys_words, keys_scales, ptab, gout, 
         pair_sums = ps.tile([P, P], F32, name="pair_sums")
         nc.tensor.transpose(pair_sums[:], turned_sb[:], ident[:])
 
-        val_scale_picked = [sb.tile([P, HALF], U8, name="val_scale_picked0", align_bytes=64),
-                            reuse.tile([P, HALF], U8, name="val_scale_picked1", offset=1088, align_bytes=64)]
+        val_scale_picked = [reuse.tile([P, HALF], U8, name="val_scale_picked%d" % h, offset=1088 + HALF * h, align_bytes=64)
+                            for h in range(HALVES)]
         gather_scales(val_scale_picked, val_scale_window, val_plane, (nc.sync,))
         val_picked = [reuse.tile([P, HALF], U16, name="val_picked%d" % h, offset=64 + 2048 * h, align_bytes=64)
                       for h in range(HALVES)]
-        grads = [product(("grads0", "turned")[h], val_picked[h][:], val_word_window, val_plane, gout_mx, h)
+        grads = [product("grads%d" % h, val_picked[h][:], val_word_window, val_plane, gout_mx, h)
                  for h in range(HALVES)]
 
         moment = sb.tile([P, G], F32, name="moment")
@@ -189,7 +188,7 @@ def tile_attend_bpagecap_kernel(tc, query, keys_words, keys_scales, ptab, gout, 
                                     weighted[h][:].rearrange("p g a b -> p g (a b)"), AXIS.X, ALU.add)
 
         share = sb.tile([P, G], F32, name="share")
-        ratio = sb.tile([P, G], F32, name="ratio")
+        ratio = reuse.tile([P, G], F32, name="ratio", offset=64 + 2048, align_bytes=64)
         root = sb.tile([P, G], F32, name="root")
         inv = sb.tile([P, G], F32, name="inv")
         inv_square = sb.tile([P, G], F32, name="inv_square")

from contextlib import ExitStack

import concourse.mybir as mybir

D, E, T, I, G, U, Q = 512, 512, 4096, 1024, 64, 512, 128
FLOPS = 2 * Q * I * (D + E)

F32 = mybir.dt.float32
BF16 = mybir.dt.bfloat16
I32 = mybir.dt.int32
U32 = mybir.dt.uint32
U16 = mybir.dt.uint16
U8 = mybir.dt.uint8
FP8X4 = mybir.dt.float8_e4m3fn_x4
FP4X4 = mybir.dt.float4_e2m1fn_x4
ALU = mybir.AluOpType
ACT = mybir.ActivationFunctionType
AXIS = mybir.AxisListType

P = 128
PACK = 4
PAGE = I // G
HALF = 512
HALVES = I // HALF
HALF_PAGES = HALF // PAGE
PAIRS = PAGE // 2
SPREAD = 8


def tile_attend_bpagecap_kernel(tc, query, keys_words, keys_scales, ptab, gout, vals_words, vals_scales, old,
                                 offs, offs2, out):
    nc = tc.nc
    with ExitStack() as ctx:
        sb = ctx.enter_context(tc.tile_pool(name="sb", bufs=1))
        reuse = ctx.enter_context(tc.tile_pool(name="reuse", bufs=1))
        late = ctx.enter_context(tc.tile_pool(name="late", bufs=1))
        ps = ctx.enter_context(tc.psum_pool(name="ps", bufs=1))

        slots = sb.tile([P, I // 16], U16, name="slots")
        pages = sb.tile([P, G // 16], U16, name="pages")
        nc.sync.dma_start(slots[:], offs)

        def half_list(h):
            cols = HALF // 16
            return slots[:, h * cols:(h + 1) * cols]

        def load_scales(window, scales):
            nc.vector.memset(window[:].bitcast(I32), 0)
            nc.sync.dma_start(window[0:P:SPREAD, :].bitcast(I32), scales[0].bitcast(I32))

        def load_words(window, words):
            nc.sync.dma_start(window[:].bitcast(I32), words[0].bitcast(I32))
            return window

        def load_rows(raw, rows):
            nc.sync.dma_start(raw[:], rows.rearrange("(p t) q -> p t q", t=PACK))
            return raw

        def empty_plane(name):
            planes = [sb.tile([P, HALF], U8, name="%s_scale_plane%d" % (name, h), align_bytes=64) for h in range(HALVES)]
            for plane in planes:
                nc.vector.memset(plane[:].bitcast(I32), 0)
            return planes

        def gather_scales(picked, window, planes, queues):
            for h in range(HALVES):
                nc.vector.tensor_copy(picked[h][:], window[:].indirect(half_list(h)))
                for quad in range(4):
                    queue = queues[quad % len(queues)]
                    queue.dma_start(planes[h][32 * quad:32 * quad + 4, :].bitcast(I32),
                                    picked[h][32 * quad:32 * quad + 32:SPREAD, :].bitcast(I32))

        def weave(name, raw):
            woven = sb.tile([P, Q, PACK], BF16, name=name + "_woven", align_bytes=64)
            nc.scalar.copy(woven[:], raw[:].rearrange("p t q -> p q t"))
            return woven

        def quantise(name, woven):
            codes = sb.tile([P, Q], U32, name=name + "_codes", align_bytes=64)
            plane = sb.tile([P, Q], U8, name=name + "_plane", align_bytes=64)
            nc.vector.quantize_mx(out=codes[:].bitcast(FP8X4), scales=plane[:],
                                  in_=woven[:].rearrange("p q t -> p (q t)"))
            return codes, plane

        def product(tag, picked, window, plane, rows, h):
            nc.vector.tensor_copy(picked, window[:].indirect(half_list(h)))
            bank = ps.tile([P, HALF], F32, name="bank", tag=tag)
            nc.tensor.matmul_mx(out=bank[:], lhsT=rows[0][:].bitcast(FP8X4), lhsT_scale=rows[1][:],
                                rhs=picked.bitcast(FP4X4), rhs_scale=plane[h][:],
                                start=True, stop=True)
            return bank

        seed = sb.tile([P, 1], F32, name="seed")
        nc.gpsimd.memset(seed[:], 0.0)
        warm = sb.tile([P, 1], F32, name="warm")
        nc.scalar.activation(warm[:], seed[:], ACT.Exp)
        key_scale_window = sb.tile([P, T], U8, name="key_scale_window", align_bytes=64)
        val_scale_window = sb.tile([P, T], U8, name="val_scale_window", align_bytes=64)
        zeros = sb.tile([P, P], F32, name="zeros", tag="zeros_then_key_words", align_bytes=64)
        nc.gpsimd.memset(zeros[:], 0.0)
        load_scales(key_scale_window, keys_scales)
        ident = sb.tile([P, P], F32, name="ident")
        nc.vector.tensor_copy(ident[:], zeros[:])
        nc.gpsimd.affine_select(out=ident[:], in_=ident[:], compare_op=ALU.not_equal, fill=1.0, base=0,
                                pattern=[[-1, P]], channel_multiplier=1)
        query_raw = load_rows(sb.tile([P, PACK, Q], F32, name="query_raw", tag="rows"), query)
        nc.sync.dma_start(pages[:], offs2)
        log_caps = sb.tile([P, U], F32, name="log_caps")
        nc.sync.dma_start(log_caps[:], ptab)
        key_word_window = load_words(
            sb.tile([P, T], U16, name="key_word_window", tag="zeros_then_key_words", align_bytes=64), keys_words)

        load_scales(val_scale_window, vals_scales)
        key_plane = empty_plane("key")
        val_plane = empty_plane("val")
        placed = sb.tile([P, U], F32, name="placed")
        nc.vector.memset(placed[:], 0.0)

        query_mx = quantise("query", weave("query", query_raw))
        log_cap = sb.tile([P, G], F32, name="log_cap")
        nc.vector.tensor_copy(log_cap[:], log_caps[:].indirect(pages[:]))
        inv_cap = sb.tile([P, G], F32, name="inv_cap")
        nc.scalar.activation(inv_cap[:], log_cap[:], ACT.Exp, scale=-1.0)

        gout_raw = load_rows(sb.tile([P, PACK, Q], F32, name="gout_raw", tag="rows"), gout)
        key_scale_picked = [late.tile([P, HALF], U8, name="key_scale_picked0", offset=2 * T - HALF // 2, align_bytes=64),
                            sb.tile([P, HALF], U8, name="key_scale_picked1", align_bytes=64)]
        gather_scales(key_scale_picked, key_scale_window, key_plane, (nc.sync, nc.scalar))
        val_word_window = load_words(late.tile([P, T], U16, name="val_word_window", offset=0, align_bytes=64), vals_words)
        old_sb = late.tile([P, U], F32, name="old_sb", offset=2 * T, align_bytes=64)
        nc.sync.dma_start(old_sb[:], old)

        key_picked = reuse.tile([P, I], U16, name="key_picked", offset=1024, align_bytes=64)
        scores = [product("scores%d" % h, key_picked[:, h * HALF:(h + 1) * HALF], key_word_window, key_plane, query_mx, h)
                  for h in range(HALVES)]
        gout_mx = quantise("gout", weave("gout", gout_raw))
        neg_max0 = sb.tile([P, 1], F32, name="neg_max0")
        nc.vector.tensor_reduce(neg_max0[:], scores[0][:], AXIS.X, ALU.max, negate=True)
        max1 = sb.tile([P, 1], F32, name="max1")
        nc.vector.tensor_reduce(max1[:], scores[1][:], AXIS.X, ALU.max)
        excess = sb.tile([P, 1], F32, name="excess")
        nc.scalar.activation(excess[:], max1[:], ACT.Relu, bias=neg_max0[:])
        neg_max = sb.tile([P, 1], F32, name="neg_max")
        nc.scalar.activation(neg_max[:], excess[:], ACT.Identity, bias=neg_max0[:], scale=-1.0)

        weights = sb.tile([P, PAIRS, G, 2], F32, name="weights")
        part_sums = sb.tile([P, 2, HALVES], F32, name="part_sums")
        for part in range(2):
            pairs = slice(part * PAIRS // 2, (part + 1) * PAIRS // 2)
            for h in range(HALVES):
                nc.scalar.activation(weights[:, pairs, h * HALF_PAGES:(h + 1) * HALF_PAGES, :],
                                     scores[h][:].rearrange("p (g a b) -> p a g b", a=PAIRS, b=2)[:, pairs],
                                     ACT.Exp, bias=neg_max[:], accum_out=part_sums[:, part, h:h + 1])
        row_sum = sb.tile([P, 1], F32, name="row_sum")
        part_copy = sb.tile([P, 2, HALVES], F32, name="part_copy")
        nc.scalar.activation(part_copy[:], part_sums[:], ACT.Identity, accum_out=row_sum[:])


        turned = ps.tile([P, P], F32, name="turned", tag="turned")
        for a in range(PAIRS):
            nc.tensor.matmul(turned[:], weights[:, a, :, :].rearrange("p g b -> p (g b)"), ident[:],
                             is_transpose=True, start=(a == 0), stop=(a == PAIRS - 1))
        turned_sb = sb.tile([P, P], F32, name="turned_sb")
        nc.scalar.copy(turned_sb[:], turned[:])
        warm_root = sb.tile([P, 1], F32, name="warm_root")
        nc.scalar.activation(warm_root[:], turned_sb[:, 0:1], ACT.Abs_reciprocal_sqrt, bias=row_sum[:])
        pair_sums = ps.tile([P, P], F32, name="pair_sums")
        nc.tensor.transpose(pair_sums[:], turned_sb[:], ident[:])

        val_scale_picked = [reuse.tile([P, HALF], U8, name="val_scale_picked%d" % h, offset=1088 + HALF * h, align_bytes=64)
                            for h in range(HALVES)]
        gather_scales(val_scale_picked, val_scale_window, val_plane, (nc.sync,))
        val_picked = [reuse.tile([P, HALF], U16, name="val_picked%d" % h, offset=64 + 2048 * h, align_bytes=64)
                      for h in range(HALVES)]
        grads = [product("grads%d" % h, val_picked[h][:], val_word_window, val_plane, gout_mx, h)
                 for h in range(HALVES)]

        moment = sb.tile([P, G], F32, name="moment")
        weighted = [sb.tile([P, HALF_PAGES, PAIRS, 2], F32, name="weighted%d" % h) for h in range(HALVES)]

        def weigh(h):
            nc.vector.tensor_tensor(weighted[h][:], grads[h][:].rearrange("p (g a b) -> p g a b", a=PAIRS, b=2),
                                    weights[:, :, h * HALF_PAGES:(h + 1) * HALF_PAGES, :].rearrange("p a g b -> p g a b"),
                                    ALU.mult)

        def sum_pages(h):
            nc.vector.tensor_reduce(moment[:, h * HALF_PAGES:(h + 1) * HALF_PAGES],
                                    weighted[h][:].rearrange("p g a b -> p g (a b)"), AXIS.X, ALU.add)

        share = sb.tile([P, G], F32, name="share")
        ratio = reuse.tile([P, G], F32, name="ratio", offset=64 + 2048, align_bytes=64)
        root = sb.tile([P, G], F32, name="root")
        inv = sb.tile([P, G], F32, name="inv")
        inv_square = sb.tile([P, G], F32, name="inv_square")
        factor = sb.tile([P, G], F32, name="factor")

        nc.vector.tensor_reduce(share[:], pair_sums[:].rearrange("p (g b) -> p g b", b=2), AXIS.X, ALU.add)
        weigh(0)
        nc.vector.tensor_tensor(ratio[:], share[:], inv_cap[:], ALU.mult)
        nc.scalar.activation(root[:], ratio[:], ACT.Abs_reciprocal_sqrt, bias=row_sum[:])
        nc.scalar.activation(inv[:], root[:], ACT.Square)
        nc.scalar.activation(inv_square[:], inv[:], ACT.Square)
        weigh(1)
        sum_pages(0)
        nc.vector.scalar_tensor_tensor(factor[:], ratio[:], 64.0, inv_square[:], ALU.mult, ALU.mult)
        sum_pages(1)
        nc.vector.tensor_tensor(placed[:].indirect(pages[:]), moment[:], factor[:], ALU.mult)

        result = sb.tile([P, U], F32, name="result")
        for h, queue in enumerate((nc.sync, nc.scalar)):
            cols = slice(h * U // 2, (h + 1) * U // 2)
            nc.vector.tensor_tensor(result[:, cols], placed[:, cols], old_sb[:, cols], ALU.add)
            queue.dma_start(out[:, cols], result[:, cols])
